import numpy as np
import ml_dtypes


def mxq(x, axis, fmt="e4m3"):
    dtype, down = {"e4m3": (ml_dtypes.float8_e4m3fn, 7), "e5m2": (ml_dtypes.float8_e5m2, 14)}[fmt]
    v = np.moveaxis(np.asarray(x, np.float32).astype(ml_dtypes.bfloat16).astype(np.float64), axis, -1)
    blocks = v.reshape(v.shape[:-1] + (-1, 32))
    amax = np.abs(blocks).max(-1, keepdims=True)
    byte = np.maximum(np.where(amax > 0, np.frexp(amax)[1] - 1 + 127, 0) - down, 1)
    scale = np.exp2(byte - 127.0)
    codes = (blocks / scale).astype(np.float32).astype(dtype).astype(np.float64)
    return np.moveaxis((codes * scale).reshape(v.shape), -1, axis)


WIDE = False


def mx_kscale(k):
    if not WIDE:
        return np.ones(k)
    levels = np.array([10, -10, 5, -5, 0])
    if k % 512:
        return np.exp2(np.random.permutation(np.resize(levels, k // 32))).repeat(32)
    a = np.empty((k // 512, 16))
    for p in range(k // 512):
        a[p, :8] = np.random.permutation(np.resize(levels, 8))
        for g in range(8):
            far = levels[np.abs(levels - a[p, g]) >= 10]
            a[p, g + 8] = far[np.random.randint(len(far))]
    return np.exp2(a.ravel()).repeat(32)


def f64(x):
    return np.asarray(x).astype(np.float64)


def striped(idx):
    return np.tile(idx.reshape(-1, 16).T, (8, 1)).astype(np.uint16)


def unstriped(offs):
    return offs[:16].T.reshape(-1).astype(np.int64)


E2M1 = np.array([0.0, 0.5, 1.0, 1.5, 2.0, 3.0, 4.0, 6.0, -0.0, -0.5, -1.0, -1.5, -2.0, -3.0, -4.0, -6.0])


def pack_weight(w, fmt):
    k, n = w.shape
    w = f64(np.asarray(w, np.float32).astype(ml_dtypes.bfloat16)).reshape(k // 32, 32, n)
    amax = np.abs(w).max(1)
    if fmt == "e4m3":
        byte = np.frexp(amax)[1] - 1 + 127 - 7
    else:
        mant, ex = np.frexp(amax / 6.0)
        byte = np.where(mant > 0.5, ex, ex - 1) + 127
    byte = np.clip(np.where(amax > 0, byte, 1), 1, 254)
    scaled = (w * np.exp2(127.0 - byte)[:, None, :]).reshape(k, n).astype(np.float32)
    by_word = np.ascontiguousarray(scaled.reshape(k // 512, 128, 4, n).transpose(0, 1, 3, 2))
    if fmt == "e4m3":
        words = by_word.astype(ml_dtypes.float8_e4m3fn).view(np.uint8)
    else:
        c = by_word.astype(ml_dtypes.float4_e2m1fn).view(np.uint8) & 0xF
        words = (c[..., 0::2] | (c[..., 1::2] << 4)).reshape(k // 512, 128, 2 * n)
    return np.ascontiguousarray(words), np.ascontiguousarray(byte.astype(np.uint8).reshape(k // 512, 16, n))


def unpack_weight(words, scales, fmt):
    g, _, n = scales.shape
    words = np.ascontiguousarray(words).reshape(g, 128, n, -1)
    if fmt == "e4m3":
        vals = words.view(ml_dtypes.float8_e4m3fn).astype(np.float64)
    else:
        nib = np.empty((g, 128, n, 4), np.uint8)
        nib[..., 0::2] = words & 0xF
        nib[..., 1::2] = words >> 4
        vals = E2M1[nib]
    vals = vals * np.repeat(np.exp2(scales.astype(np.float64) - 127.0), 8, axis=1)[..., None]
    return vals.transpose(0, 1, 3, 2).reshape(g * 512, n)


def relu2(v):
    return np.maximum(v, 0.0) ** 2


K, T, E, C, N = 1024, 640, 20, 128, 128
TOP = 4


def by_expert(wq, xq):
    return np.concatenate([wq[e].T @ xq[:, e * C:(e + 1) * C] for e in range(E)], axis=1)


def setup_inputs():
    n = np.random.standard_normal
    s = mx_kscale(K)[:, None]
    deal = np.repeat(np.arange(E), C).reshape(TOP, T)[:, np.random.permutation(T)]
    deal = np.take_along_axis(deal, np.argsort(np.random.rand(TOP, T), axis=0), axis=0)
    for _ in range(8):
        s_, t_ = np.random.permutation(T).reshape(2, -1); r = np.random.randint(TOP, size=T // 2); x, y = deal[r, s_].copy(), deal[r, t_].copy()
        ok = ~((deal[:, s_] == y).any(0) | (deal[:, t_] == x).any(0)); deal[r[ok], s_[ok]] = y[ok]; deal[r[ok], t_[ok]] = x[ok]
    order = np.lexsort((np.random.rand(TOP * T), deal.reshape(-1)))
    slot_token = order % T; pos = np.empty(TOP * T, np.int64); pos[order] = np.arange(TOP * T); pos = pos.reshape(TOP, T)
    g = np.random.uniform(0.5, 1.5, (TOP, T)); g = g / g.sum(0)
    w = [pack_weight(m, "e2m1") for m in n((E + 1, K, N)) / np.sqrt(K) / s[None]]
    return {
        "xT": (n((K, T)) * s).astype(np.float32),
        "w_words": np.stack([m[0] for m in w]),
        "w_scales": np.stack([m[1] for m in w]),
        "b": (0.3 * n((N, E + 1))).astype(np.float32),
        "gate": np.stack([np.tile(r, (N, 1)) for r in g]).astype(np.float32),
        "offs": striped(slot_token),
        "pos1": striped(pos[0]),
        "pos2": striped(pos[1]),
        "pos3": striped(pos[2]),
        "pos4": striped(pos[3]),
    }


def reference(xT, w_words, w_scales, b, gate, offs, pos1, pos2, pos3, pos4):
    idx = unstriped(offs)
    w = np.stack([unpack_weight(w_words[e], w_scales[e], "e2m1") for e in range(E + 1)])
    wq = w
    xs = mxq(f64(xT), 0, "e4m3")
    ys = relu2((wq[E].T @ xs) + f64(b)[:, E:])
    xq = mxq(f64(xT)[:, idx], 0, "e4m3")
    y = by_expert(w, xq)
    y = relu2(y + np.repeat(f64(b)[:, :E], C, axis=1))
    return ys + sum(f64(gate[r]) * y[:, unstriped(p)] for r, p in enumerate((pos1, pos2, pos3, pos4)))

@@ -1,0 +1,180 @@
+from contextlib import ExitStack
+
+import concourse.mybir as mybir
+
+K, T, E, C, N = 1024, 640, 20, 128, 128
+TOP = 4
+FLOPS = 2 * K * N * (E * C + T)
+
+F32 = mybir.dt.float32
+BF16 = mybir.dt.bfloat16
+I32 = mybir.dt.int32
+U32 = mybir.dt.uint32
+U16 = mybir.dt.uint16
+U8 = mybir.dt.uint8
+FP8X4 = mybir.dt.float8_e4m3fn_x4
+FP4X4 = mybir.dt.float4_e2m1fn_x4
+ACT = mybir.ActivationFunctionType
+ALU = mybir.AluOpType
+
+P = 128
+PASSES = 2
+WINDOW = 704
+CHUNKS = [512, 512, 512, 512, 256, 256]
+
+
+def tile_moe_shr_lin_relu2_kernel(
+    tc, xT, w_words, w_scales, b, gate, offs, pos1, pos2, pos3, pos4, out
+):
+    nc = tc.nc
+    with ExitStack() as ctx:
+        keep = ctx.enter_context(tc.tile_pool(name="keep", bufs=1))
+        psum = ctx.enter_context(tc.psum_pool(name="psum", bufs=1))
+
+        slot_list = keep.tile([P, E * C // 16], U16, name="slot_list")
+        back_lists = [keep.tile([P, T // 16], U16, name="back_list%d" % r) for r in range(TOP)]
+        raw = keep.tile([P, 4, 2, T], F32, name="raw")
+        pairs = keep.tile([P, 4, 2 * WINDOW], BF16, name="pairs", align_bytes=64)
+        weights = keep.tile([P, (E + 1) * PASSES, 2 * N], U8, name="weights", align_bytes=64)
+        weight_scales = keep.tile([P, (E + 1) * PASSES, N], U8, name="weight_scales", align_bytes=64)
+        bias = keep.tile([P, E + 1], F32, name="bias")
+        gates = keep.tile([P, TOP, T], F32, name="gates")
+        y = keep.tile([P, E * C], F32, name="y")
+
+        rows = xT.rearrange("(a p u j) t -> p a u j t", a=PASSES, u=2, j=2)
+        half = T // 2
+        for t0 in (0, half):
+            nc.sync.dma_start(out=raw[:, 0, :, t0 : t0 + half], in_=rows[:, 0, 0, :, t0 : t0 + half])
+        nc.sync.dma_start(slot_list[:], offs)
+        for q in range(1, 4):
+            nc.sync.dma_start(out=raw[:, q], in_=rows[:, q // 2, q % 2])
+
+        nc.vector.memset(pairs[:, :, 2 * T :].bitcast(U32), 0)
+        nc.vector.memset(weight_scales[:].rearrange("p g n -> p (g n)").bitcast(I32), 0)
+        scale_rows = w_scales.rearrange("e a q n -> q (e a) n").bitcast(I32)
+        for quad in range(4):
+            nc.sync.dma_start(
+                out=weight_scales[32 * quad : 32 * quad + 4].bitcast(I32), in_=scale_rows[4 * quad : 4 * quad + 4]
+            )
+        word_rows = w_words.rearrange("e a p c -> p (e a) c").bitcast(I32)
+        for g0, g1 in ((0, 16), (16, 32), (32, 42)):
+            nc.sync.dma_start(out=weights[:, g0:g1].bitcast(I32), in_=word_rows[:, g0:g1])
+        nc.sync.dma_start(out=bias[:], in_=b)
+        for r, pos in enumerate((pos1, pos2, pos3, pos4)):
+            nc.sync.dma_start(back_lists[r][:], pos)
+        nc.sync.dma_start(out=gates[:], in_=gate.rearrange("r p t -> p r t"))
+
+        def cast_args(q, t0, t1):
+            return (
+                pairs[:, q, 2 * t0 : 2 * t1].rearrange("p (t j) -> p t j", j=2),
+                raw[:, q, :, t0:t1].rearrange("p j t -> p t j"),
+            )
+
+        for t0 in (0, half):
+            nc.vector.tensor_copy(*cast_args(0, t0, t0 + half))
+        for q in range(1, 4):
+            nc.scalar.copy(*cast_args(q, 0, T))
+
+        starts = [sum(CHUNKS[:c]) for c in range(len(CHUNKS))]
+        picked = [keep.tile([P, 4, 2 * s], BF16, name="picked%d" % c) for c, s in enumerate(CHUNKS)]
+        widths = CHUNKS + [T]
+        quads = [keep.tile([P, PASSES, 4 * s], BF16, name="quads%d" % c, align_bytes=64) for c, s in enumerate(widths)]
+        codes = [keep.tile([P, PASSES * s], U32, name="codes%d" % c, align_bytes=64) for c, s in enumerate(widths)]
+        scales = [keep.tile([P, PASSES * s], U8, name="scales%d" % c, align_bytes=64) for c, s in enumerate(widths)]
+        shared = len(CHUNKS)
+
+        def gather(c, q):
+            lo, hi = starts[c] // 16, (starts[c] + CHUNKS[c]) // 16
+            nc.vector.tensor_copy(picked[c][:, q].bitcast(U32), pairs[:, q].bitcast(U32).indirect(slot_list[:, lo:hi]))
+
+        def interleave(c, a):
+            src = pairs[:, 2 * a : 2 * a + 2, : 2 * T] if c == shared else picked[c][:, 2 * a : 2 * a + 2]
+            nc.scalar.copy(
+                quads[c][:, a].bitcast(F32).rearrange("p (s u) -> p s u", u=2),
+                src.bitcast(F32).rearrange("p u s -> p s u"),
+            )
+
+        def quantize(c, lo, hi):
+            nc.vector.quantize_mx(
+                out=codes[c][:, lo:hi].bitcast(FP8X4),
+                scales=scales[c][:, lo:hi],
+                in_=quads[c][:].rearrange("p a s -> p (a s)")[:, 4 * lo : 4 * hi],
+            )
+
+        def product(acc, e, c, lo, hi):
+            for a in range(PASSES):
+                cols = slice(a * widths[c] + lo, a * widths[c] + hi)
+                nc.tensor.matmul_mx(
+                    out=acc,
+                    lhsT=weights[:, PASSES * e + a].bitcast(FP4X4),
+                    lhsT_scale=weight_scales[:, PASSES * e + a],
+                    rhs=codes[c][:, cols].bitcast(FP8X4),
+                    rhs_scale=scales[c][:, cols],
+                    start=(a == 0),
+                    stop=(a == PASSES - 1),
+                )
+
+        def experts(c):
+            s = CHUNKS[c]
+            acc = psum.tile([P, s], F32, name="acc%d" % c)
+            rect = keep.tile([P, s], F32, name="rect%d" % c)
+            first = starts[c] // C
+            for i in range(s // C):
+                product(acc[:, i * C : (i + 1) * C], first + i, c, i * C, (i + 1) * C)
+            for i in range(s // C):
+                cols = slice(i * C, (i + 1) * C)
+                nc.scalar.activation(rect[:, cols], acc[:, cols], ACT.Relu, bias=bias[:, first + i : first + i + 1])
+            nc.scalar.activation(y[:, starts[c] : starts[c] + s], rect[:], ACT.Square)
+
+        def finish(c):
+            for a in range(PASSES):
+                quantize(c, a * CHUNKS[c], (a + 1) * CHUNKS[c])
+            experts(c)
+
+        for q in range(4):
+            gather(0, q)
+            gather(1, q)
+            if q % 2 == 1:
+                interleave(0, q // 2)
+                interleave(1, q // 2)
+        for c in range(2, len(CHUNKS)):
+            for a in range(PASSES):
+                gather(c, 2 * a)
+                gather(c, 2 * a + 1)
+                interleave(c, a)
+            if c == 2:
+                finish(0)
+            if c in (2, 3):
+                interleave(shared, c - 2)
+            finish(c - 1)
+        finish(len(CHUNKS) - 1)
+
+        quantize(shared, 0, 1024)
+        quantize(shared, 1024, 1280)
+        ys = keep.tile([P, T], F32, name="ys")
+        rect_shared = keep.tile([P, T], F32, name="rect_shared")
+        for lo, hi in ((0, 512), (512, T)):
+            acc = psum.tile([P, hi - lo], F32, name="acc_shared%d" % lo)
+            product(acc[:], E, shared, lo, hi)
+            nc.scalar.activation(rect_shared[:, lo:hi], acc[:], ACT.Relu, bias=bias[:, E : E + 1])
+        nc.scalar.activation(ys[:], rect_shared[:], ACT.Square)
+
+        terms = [keep.tile([P, T], F32, name="term%d" % r) for r in range(TOP)]
+        sums = [keep.tile([P, T], F32, name="sum%d" % r) for r in range(TOP)]
+
+        def fetch(r):
+            nc.vector.tensor_tensor(terms[r][:], y[:].indirect(back_lists[r][:]), gates[:, r], ALU.mult)
+
+        fetch(0)
+        fetch(1)
+        nc.vector.tensor_tensor(sums[0][:], terms[0][:], ys[:], ALU.add)
+        fetch(2)
+        nc.vector.tensor_tensor(sums[1][:], sums[0][:], terms[1][:], ALU.add)
+        fetch(3)
+        for t0 in (0, half):
+            cols = slice(t0, t0 + half)
+            nc.vector.tensor_tensor(sums[2][:, cols], sums[1][:, cols], terms[2][:, cols], ALU.add)
+        for t0 in (0, half):
+            cols = slice(t0, t0 + half)
+            nc.vector.tensor_tensor(sums[3][:, cols], sums[2][:, cols], terms[3][:, cols], ALU.add)
+            nc.sync.dma_start(out=out[:, cols], in_=sums[3][:, cols])

@@ -21,6 +21,8 @@ P = 128
 PASSES = 2
 WINDOW = 704
 CHUNKS = [512, 512, 512, 512, 256, 256]
+SCALAR_EXPERTS = 16
+GPSIMD_UNITS = [(0, 0), (1, 0), (0, 1), (1, 1), (2, 1), (3, 1), (6, 0), (6, 1)]
 
 
 def tile_moe_shr_lin_relu2_kernel(
@@ -72,8 +74,11 @@ def tile_moe_shr_lin_relu2_kernel(
 
         for t0 in (0, half):
             nc.vector.tensor_copy(*cast_args(0, t0, t0 + half))
-        for q in range(1, 4):
-            nc.scalar.copy(*cast_args(q, 0, T))
+        singles = keep.tile([P, 2, T], BF16, name="singles")
+        nc.scalar.copy(singles[:, 0], raw[:, 1, 0])
+        nc.gpsimd.tensor_scalar(singles[:, 1], raw[:, 1, 1], 1.0, 0.0, ALU.mult, ALU.add)
+        for q in (2, 3, 1):
+            nc.gpsimd.tensor_scalar(*cast_args(q, 0, T), 1.0, 0.0, ALU.mult, ALU.add)
 
         starts = [sum(CHUNKS[:c]) for c in range(len(CHUNKS))]
         picked = [keep.tile([P, 4, 2 * s], BF16, name="picked%d" % c) for c, s in enumerate(CHUNKS)]
@@ -84,14 +89,32 @@ def tile_moe_shr_lin_relu2_kernel(
         shared = len(CHUNKS)
 
         def gather(c, q):
-            lo, hi = starts[c] // 16, (starts[c] + CHUNKS[c]) // 16
-            nc.vector.tensor_copy(picked[c][:, q].bitcast(U32), pairs[:, q].bitcast(U32).indirect(slot_list[:, lo:hi]))
+            first = starts[c]
+            if q == 1:
+                for s0 in range(first, min(starts[c] + CHUNKS[c], SCALAR_EXPERTS * C), C):
+                    slots = picked[c][:, q].rearrange("p (s j) -> p s j", j=2)[:, s0 - starts[c] : s0 - starts[c] + C]
+                    for j in range(2):
+                        window = singles[:, j].indirect(slot_list[:, s0 // 16 : (s0 + C) // 16])
+                        nc.scalar.activation(slots[:, :, j], window, ACT.Copy)
+                    first = s0 + C
+            last = starts[c] + CHUNKS[c]
+            if first < last:
+                nc.vector.tensor_copy(
+                    picked[c][:, q].bitcast(U32)[:, first - starts[c] :],
+                    pairs[:, q].bitcast(U32).indirect(slot_list[:, first // 16 : last // 16]),
+                )
 
         def interleave(c, a):
-            src = pairs[:, 2 * a : 2 * a + 2, : 2 * T] if c == shared else picked[c][:, 2 * a : 2 * a + 2]
+            if (c, a) in GPSIMD_UNITS:
+                src = pairs[:, 2 * a : 2 * a + 2, : 2 * T] if c == shared else picked[c][:, 2 * a : 2 * a + 2]
+                nc.gpsimd.tensor_copy(
+                    quads[c][:, a].bitcast(U32).rearrange("p (s u) -> p s u", u=2),
+                    src.bitcast(U32).rearrange("p u s -> p s u"),
+                )
+                return
             nc.scalar.copy(
                 quads[c][:, a].bitcast(F32).rearrange("p (s u) -> p s u", u=2),
-                src.bitcast(F32).rearrange("p u s -> p s u"),
+                picked[c][:, 2 * a : 2 * a + 2].bitcast(F32).rearrange("p u s -> p s u"),
             )
 
         def quantize(c, lo, hi):
@@ -126,31 +149,31 @@ def tile_moe_shr_lin_relu2_kernel(
                 nc.scalar.activation(rect[:, cols], acc[:, cols], ACT.Relu, bias=bias[:, first + i : first + i + 1])
             nc.scalar.activation(y[:, starts[c] : starts[c] + s], rect[:], ACT.Square)
 
-        def finish(c):
-            for a in range(PASSES):
-                quantize(c, a * CHUNKS[c], (a + 1) * CHUNKS[c])
-            experts(c)
+        def quantize_chunk(c):
+            quantize(c, 0, PASSES * CHUNKS[c])
 
-        for q in range(4):
-            gather(0, q)
-            gather(1, q)
-            if q % 2 == 1:
-                interleave(0, q // 2)
-                interleave(1, q // 2)
-        for c in range(2, len(CHUNKS)):
+        interleave(shared, 1)
+        interleave(shared, 0)
+        for c in range(4):
+            gather(c, 1)
+        for c, q in ((0, 0), (1, 0), (2, 0), (0, 2), (1, 2), (0, 3), (1, 3), (2, 2), (2, 3), (3, 0), (3, 2), (3, 3)):
+            gather(c, q)
+        for c in range(4):
             for a in range(PASSES):
+                interleave(c, a)
+        for c in (4, 5):
+            for a in range(PASSES):
+                quantize_chunk(2 * (c - 4) + a)
                 gather(c, 2 * a)
                 gather(c, 2 * a + 1)
                 interleave(c, a)
-            if c == 2:
-                finish(0)
-            if c in (2, 3):
-                interleave(shared, c - 2)
-            finish(c - 1)
-        finish(len(CHUNKS) - 1)
-
-        quantize(shared, 0, 1024)
+        quantize(shared, 0, 512)
+        quantize_chunk(4)
+        quantize_chunk(5)
+        quantize(shared, 512, 1024)
         quantize(shared, 1024, 1280)
+        for c in range(len(CHUNKS)):
+            experts(c)
         ys = keep.tile([P, T], F32, name="ys")
         rect_shared = keep.tile([P, T], F32, name="rect_shared")
         for lo, hi in ((0, 512), (512, T)):

@@ -1,6 +1,7 @@
 from contextlib import ExitStack
 
 import concourse.mybir as mybir
+from concourse.masks import make_identity
 
 K, T, E, C, N = 1024, 640, 20, 128, 128
 TOP = 4
@@ -21,8 +22,7 @@ P = 128
 PASSES = 2
 WINDOW = 704
 CHUNKS = [512, 512, 512, 512, 256, 256]
-SCALAR_EXPERTS = 16
-GPSIMD_UNITS = [(0, 0), (1, 0), (0, 1), (1, 1), (2, 1), (3, 1), (6, 0), (6, 1)]
+SCALAR_EXPERTS = 18
 
 
 def tile_moe_shr_lin_relu2_kernel(
@@ -44,9 +44,9 @@ def tile_moe_shr_lin_relu2_kernel(
         y = keep.tile([P, E * C], F32, name="y")
 
         rows = xT.rearrange("(a p u j) t -> p a u j t", a=PASSES, u=2, j=2)
-        half = T // 2
-        for t0 in (0, half):
-            nc.sync.dma_start(out=raw[:, 0, :, t0 : t0 + half], in_=rows[:, 0, 0, :, t0 : t0 + half])
+        head_pieces = ((0, 448), (448, T))
+        for t0, t1 in head_pieces:
+            nc.sync.dma_start(out=raw[:, 0, :, t0:t1], in_=rows[:, 0, 0, :, t0:t1])
         nc.sync.dma_start(slot_list[:], offs)
         for q in range(1, 4):
             nc.sync.dma_start(out=raw[:, q], in_=rows[:, q // 2, q % 2])
@@ -72,132 +72,201 @@ def tile_moe_shr_lin_relu2_kernel(
                 raw[:, q, :, t0:t1].rearrange("p j t -> p t j"),
             )
 
-        for t0 in (0, half):
-            nc.vector.tensor_copy(*cast_args(0, t0, t0 + half))
+        for t0, t1 in head_pieces:
+            nc.vector.tensor_copy(*cast_args(0, t0, t1))
         singles = keep.tile([P, 2, T], BF16, name="singles")
         nc.scalar.copy(singles[:, 0], raw[:, 1, 0])
         nc.gpsimd.tensor_scalar(singles[:, 1], raw[:, 1, 1], 1.0, 0.0, ALU.mult, ALU.add)
         for q in (2, 3, 1):
             nc.gpsimd.tensor_scalar(*cast_args(q, 0, T), 1.0, 0.0, ALU.mult, ALU.add)
 
+        identity = keep.tile([P, P], F32, name="identity")
+        make_identity(nc, identity[:])
+
         starts = [sum(CHUNKS[:c]) for c in range(len(CHUNKS))]
-        picked = [keep.tile([P, 4, 2 * s], BF16, name="picked%d" % c) for c, s in enumerate(CHUNKS)]
-        widths = CHUNKS + [T]
-        quads = [keep.tile([P, PASSES, 4 * s], BF16, name="quads%d" % c, align_bytes=64) for c, s in enumerate(widths)]
-        codes = [keep.tile([P, PASSES * s], U32, name="codes%d" % c, align_bytes=64) for c, s in enumerate(widths)]
-        scales = [keep.tile([P, PASSES * s], U8, name="scales%d" % c, align_bytes=64) for c, s in enumerate(widths)]
-        shared = len(CHUNKS)
+        last = len(CHUNKS) - 1
+        picked, quads, codes, scales = {}, {}, {}, {}
+
+        def open_chunk(c, passes, tag):
+            tile = keep.tile([P, 2 * len(passes), 2 * CHUNKS[c]], BF16, name="picked%d_%d" % (c, passes[0]), tag=tag)
+            for i, a in enumerate(passes):
+                picked[c, a] = tile[:, 2 * i : 2 * i + 2]
+            if 0 in passes:
+                quads[c] = keep.tile(
+                    [P, PASSES, 4 * CHUNKS[c]], BF16, name="quads%d" % c, tag="quads%d" % c, align_bytes=64
+                )
+
+        def on_scalar(c):
+            return min(CHUNKS[c], max(0, SCALAR_EXPERTS * C - starts[c]))
 
         def gather(c, q):
-            first = starts[c]
-            if q == 1:
-                for s0 in range(first, min(starts[c] + CHUNKS[c], SCALAR_EXPERTS * C), C):
-                    slots = picked[c][:, q].rearrange("p (s j) -> p s j", j=2)[:, s0 - starts[c] : s0 - starts[c] + C]
-                    for j in range(2):
-                        window = singles[:, j].indirect(slot_list[:, s0 // 16 : (s0 + C) // 16])
-                        nc.scalar.activation(slots[:, :, j], window, ACT.Copy)
-                    first = s0 + C
-            last = starts[c] + CHUNKS[c]
-            if first < last:
-                nc.vector.tensor_copy(
-                    picked[c][:, q].bitcast(U32)[:, first - starts[c] :],
-                    pairs[:, q].bitcast(U32).indirect(slot_list[:, first // 16 : last // 16]),
-                )
-
-        def interleave(c, a):
-            if (c, a) in GPSIMD_UNITS:
-                src = pairs[:, 2 * a : 2 * a + 2, : 2 * T] if c == shared else picked[c][:, 2 * a : 2 * a + 2]
-                nc.gpsimd.tensor_copy(
-                    quads[c][:, a].bitcast(U32).rearrange("p (s u) -> p s u", u=2),
-                    src.bitcast(U32).rearrange("p u s -> p s u"),
-                )
-                return
-            nc.scalar.copy(
-                quads[c][:, a].bitcast(F32).rearrange("p (s u) -> p s u", u=2),
-                picked[c][:, 2 * a : 2 * a + 2].bitcast(F32).rearrange("p u s -> p s u"),
+            skip = on_scalar(c) if q == 1 else 0
+            first, end = starts[c] + skip, starts[c] + CHUNKS[c]
+            nc.vector.tensor_copy(
+                picked[c, q // 2][:, q % 2].bitcast(U32)[:, skip:],
+                pairs[:, q].bitcast(U32).indirect(slot_list[:, first // 16 : end // 16]),
             )
 
-        def quantize(c, lo, hi):
-            nc.vector.quantize_mx(
-                out=codes[c][:, lo:hi].bitcast(FP8X4),
-                scales=scales[c][:, lo:hi],
-                in_=quads[c][:].rearrange("p a s -> p (a s)")[:, 4 * lo : 4 * hi],
-            )
+        def gather_singles(c):
+            slots = picked[c, 0][:, 1].rearrange("p (s j) -> p s j", j=2)
+            for s0 in range(0, on_scalar(c), C):
+                first = starts[c] + s0
+                for j in range(2):
+                    window = singles[:, j].indirect(slot_list[:, first // 16 : (first + C) // 16])
+                    nc.scalar.activation(slots[:, s0 : s0 + C, j], window, ACT.Copy)
 
-        def product(acc, e, c, lo, hi):
+        def interleave(copy, word, dst, src):
+            copy(dst.bitcast(word).rearrange("p (s u) -> p s u", u=2), src.bitcast(word).rearrange("p u s -> p s u"))
+
+        def interleave_scalar(c, a):
+            interleave(nc.scalar.copy, F32, quads[c][:, a], picked[c, a])
+
+        def interleave_gpsimd(c, a):
+            interleave(nc.gpsimd.tensor_copy, U32, quads[c][:, a], picked[c, a])
+
+        def interleave_vector(c, a):
+            interleave(nc.vector.tensor_copy, I32, quads[c][:, a], picked[c, a])
+
+        def operand_tiles(key, width, tag):
+            codes[key] = keep.tile([P, PASSES * width], U32, name="codes%s" % key, tag=tag, align_bytes=64)
+            scales[key] = keep.tile([P, PASSES * width], U8, name="scales%s" % key, align_bytes=64)
+
+        def quantize(key, lo, hi, values):
+            nc.vector.quantize_mx(out=codes[key][:, lo:hi].bitcast(FP8X4), scales=scales[key][:, lo:hi], in_=values)
+
+        def quantize_chunk(c):
+            operand_tiles(c, CHUNKS[c], "codes%d" % c)
+            quantize(c, 0, PASSES * CHUNKS[c], quads[c][:].rearrange("p a s -> p (a s)"))
+
+        def product(acc, e, key, width, lo, hi):
             for a in range(PASSES):
-                cols = slice(a * widths[c] + lo, a * widths[c] + hi)
+                cols = slice(a * width + lo, a * width + hi)
                 nc.tensor.matmul_mx(
                     out=acc,
                     lhsT=weights[:, PASSES * e + a].bitcast(FP4X4),
                     lhsT_scale=weight_scales[:, PASSES * e + a],
-                    rhs=codes[c][:, cols].bitcast(FP8X4),
-                    rhs_scale=scales[c][:, cols],
+                    rhs=codes[key][:, cols].bitcast(FP8X4),
+                    rhs_scale=scales[key][:, cols],
                     start=(a == 0),
                     stop=(a == PASSES - 1),
                 )
 
         def experts(c):
             s = CHUNKS[c]
-            acc = psum.tile([P, s], F32, name="acc%d" % c)
+            acc = psum.tile([P, s], F32, name="acc%d" % c, tag="bank%d" % c)
             rect = keep.tile([P, s], F32, name="rect%d" % c)
             first = starts[c] // C
             for i in range(s // C):
-                product(acc[:, i * C : (i + 1) * C], first + i, c, i * C, (i + 1) * C)
+                product(acc[:, i * C : (i + 1) * C], first + i, c, s, i * C, (i + 1) * C)
             for i in range(s // C):
                 cols = slice(i * C, (i + 1) * C)
                 nc.scalar.activation(rect[:, cols], acc[:, cols], ACT.Relu, bias=bias[:, first + i : first + i + 1])
             nc.scalar.activation(y[:, starts[c] : starts[c] + s], rect[:], ACT.Square)
 
-        def quantize_chunk(c):
-            quantize(c, 0, PASSES * CHUNKS[c])
+        shared_quads = {}
 
-        interleave(shared, 1)
-        interleave(shared, 0)
-        for c in range(4):
-            gather(c, 1)
-        for c, q in ((0, 0), (1, 0), (2, 0), (0, 2), (1, 2), (0, 3), (1, 3), (2, 2), (2, 3), (3, 0), (3, 2), (3, 3)):
+        def lay_out_shared(a, tag):
+            shared_quads[a] = keep.tile([P, 4 * T], BF16, name="shared_quads%d" % a, tag=tag, align_bytes=64)
+            interleave(nc.gpsimd.tensor_copy, U32, shared_quads[a][:], pairs[:, 2 * a : 2 * a + 2, : 2 * T])
+
+        for c in range(3):
+            open_chunk(c, (0, 1), "picked%d" % c)
+        lay_out_shared(0, "shared_quads0")
+        for c, q in ((0, 0), (1, 0), (2, 0), (0, 2), (1, 2), (0, 3), (1, 3), (2, 2), (2, 3)):
             gather(c, q)
-        for c in range(4):
-            for a in range(PASSES):
-                interleave(c, a)
-        for c in (4, 5):
-            for a in range(PASSES):
-                quantize_chunk(2 * (c - 4) + a)
-                gather(c, 2 * a)
-                gather(c, 2 * a + 1)
-                interleave(c, a)
-        quantize(shared, 0, 512)
+            if q == 3:
+                interleave_gpsimd(c, 1)
+        gather_singles(0)
+        gather_singles(1)
+        interleave_scalar(0, 0)
+        gather_singles(2)
+        interleave_scalar(1, 0)
+
+        quantize_chunk(0)
+        lay_out_shared(1, "quads0")
+        open_chunk(3, (0, 1), "picked0")
+        for q in (0, 2, 3):
+            gather(3, q)
+        interleave_gpsimd(3, 1)
+        gather_singles(3)
+        interleave_scalar(2, 0)
+        interleave_scalar(3, 0)
+
+        quantize_chunk(1)
+        open_chunk(4, (0, 1), "picked1")
+        for q in (0, 2, 3):
+            gather(4, q)
+        interleave_gpsimd(4, 1)
+        gather_singles(4)
+        experts(0)
+        interleave_scalar(4, 0)
+
+        quantize_chunk(2)
+        open_chunk(5, (0,), "picked2")
+        gather(5, 0)
+        gather(5, 1)
+        interleave_gpsimd(5, 0)
+        experts(1)
+
+        quantize_chunk(3)
+        open_chunk(5, (1,), "picked0")
+        gather(5, 2)
+        gather(5, 3)
         quantize_chunk(4)
-        quantize_chunk(5)
-        quantize(shared, 512, 1024)
-        quantize(shared, 1024, 1280)
-        for c in range(len(CHUNKS)):
+        interleave_vector(5, 1)
+        operand_tiles(last, CHUNKS[last], "codes%d" % last)
+        for a in range(PASSES):
+            quantize(last, a * CHUNKS[last], (a + 1) * CHUNKS[last], quads[last][:, a])
+        for c in range(2, len(CHUNKS)):
             experts(c)
+
+        operand_tiles("shared", T, "codes4")
+        for a in range(PASSES):
+            for lo, hi in ((0, 512), (512, T)):
+                quantize("shared", a * T + lo, a * T + hi, shared_quads[a][:, 4 * lo : 4 * hi])
         ys = keep.tile([P, T], F32, name="ys")
         rect_shared = keep.tile([P, T], F32, name="rect_shared")
-        for lo, hi in ((0, 512), (512, T)):
-            acc = psum.tile([P, hi - lo], F32, name="acc_shared%d" % lo)
-            product(acc[:], E, shared, lo, hi)
+        for i, (lo, hi) in enumerate(((0, 512), (512, T))):
+            acc = psum.tile([P, hi - lo], F32, name="acc_shared%d" % i, tag="bank%d" % (6 + i))
+            product(acc[:], E, "shared", T, lo, hi)
             nc.scalar.activation(rect_shared[:, lo:hi], acc[:], ACT.Relu, bias=bias[:, E : E + 1])
-        nc.scalar.activation(ys[:], rect_shared[:], ACT.Square)
+        token_pieces = ((0, 384), (384, T))
+        for lo, hi in token_pieces:
+            nc.scalar.activation(ys[:, lo:hi], rect_shared[:, lo:hi], ACT.Square)
 
         terms = [keep.tile([P, T], F32, name="term%d" % r) for r in range(TOP)]
-        sums = [keep.tile([P, T], F32, name="sum%d" % r) for r in range(TOP)]
 
-        def fetch(r):
-            nc.vector.tensor_tensor(terms[r][:], y[:].indirect(back_lists[r][:]), gates[:, r], ALU.mult)
+        def fetch(r, lo, hi):
+            window = y[:].indirect(back_lists[r][:, lo // 16 : hi // 16])
+            nc.vector.tensor_tensor(terms[r][:, lo:hi], window, gates[:, r, lo:hi], ALU.mult)
 
-        fetch(0)
-        fetch(1)
-        nc.vector.tensor_tensor(sums[0][:], terms[0][:], ys[:], ALU.add)
-        fetch(2)
-        nc.vector.tensor_tensor(sums[1][:], sums[0][:], terms[1][:], ALU.add)
-        fetch(3)
-        for t0 in (0, half):
-            cols = slice(t0, t0 + half)
-            nc.vector.tensor_tensor(sums[2][:, cols], sums[1][:, cols], terms[2][:, cols], ALU.add)
-        for t0 in (0, half):
-            cols = slice(t0, t0 + half)
-            nc.vector.tensor_tensor(sums[3][:, cols], sums[2][:, cols], terms[3][:, cols], ALU.add)
-            nc.sync.dma_start(out=out[:, cols], in_=sums[3][:, cols])
+        partial = keep.tile([P, T], F32, name="partial")
+        result = keep.tile([P, T], F32, name="result")
+        addends = [terms[0], terms[1], ys, terms[2]]
+        backs = []
+        for i, (lo, hi) in enumerate(token_pieces):
+            for r in range(TOP - 1):
+                fetch(r, lo, hi)
+            blocks = range(lo // P, hi // P)
+            turned = {k: psum.tile([P, P], F32, name="turned%d" % k, tag="bank%d" % k) for k in blocks}
+            for n, addend in enumerate(addends):
+                for k in blocks:
+                    nc.tensor.matmul(
+                        turned[k][:],
+                        lhsT=addend[:, k * P : (k + 1) * P],
+                        rhs=identity[:],
+                        start=(n == 0),
+                        stop=(n == len(addends) - 1),
+                        is_transpose=True,
+                    )
+            for k in blocks:
+                nc.scalar.copy(partial[:, k * P : (k + 1) * P], turned[k][:])
+            back = psum.tile([P, hi - lo], F32, name="back%d" % i, tag="bank%d" % (6 + i))
+            for t0 in range(lo, hi, P):
+                nc.tensor.transpose(back[:, t0 - lo : t0 - lo + P], partial[:, t0 : t0 + P], identity[:])
+            backs.append(back)
+        for lo, hi in token_pieces:
+            fetch(TOP - 1, lo, hi)
+        for back, (lo, hi) in zip(backs, token_pieces):
+            nc.vector.tensor_tensor(result[:, lo:hi], back[:], terms[TOP - 1][:, lo:hi], ALU.add)
+            nc.sync.dma_start(out=out[:, lo:hi], in_=result[:, lo:hi])

@@ -22,7 +22,7 @@ P = 128
 PASSES = 2
 WINDOW = 704
 CHUNKS = [512, 512, 512, 512, 256, 256]
-SCALAR_EXPERTS = 18
+SCALAR_EXPERTS = 14
 
 
 def tile_moe_shr_lin_relu2_kernel(
@@ -35,7 +35,7 @@ def tile_moe_shr_lin_relu2_kernel(
 
         slot_list = keep.tile([P, E * C // 16], U16, name="slot_list")
         back_lists = [keep.tile([P, T // 16], U16, name="back_list%d" % r) for r in range(TOP)]
-        raw = keep.tile([P, 4, 2, T], F32, name="raw")
+        raw = [keep.tile([P, 2, T], F32, name="raw%d" % q, tag="raw%d" % q) for q in range(4)]
         pairs = keep.tile([P, 4, 2 * WINDOW], BF16, name="pairs", align_bytes=64)
         weights = keep.tile([P, (E + 1) * PASSES, 2 * N], U8, name="weights", align_bytes=64)
         weight_scales = keep.tile([P, (E + 1) * PASSES, N], U8, name="weight_scales", align_bytes=64)
@@ -46,10 +46,10 @@ def tile_moe_shr_lin_relu2_kernel(
         rows = xT.rearrange("(a p u j) t -> p a u j t", a=PASSES, u=2, j=2)
         head_pieces = ((0, 448), (448, T))
         for t0, t1 in head_pieces:
-            nc.sync.dma_start(out=raw[:, 0, :, t0:t1], in_=rows[:, 0, 0, :, t0:t1])
+            nc.sync.dma_start(out=raw[0][:, :, t0:t1], in_=rows[:, 0, 0, :, t0:t1])
         nc.sync.dma_start(slot_list[:], offs)
         for q in range(1, 4):
-            nc.sync.dma_start(out=raw[:, q], in_=rows[:, q // 2, q % 2])
+            nc.sync.dma_start(out=raw[q][:], in_=rows[:, q // 2, q % 2])
 
         nc.vector.memset(pairs[:, :, 2 * T :].bitcast(U32), 0)
         nc.vector.memset(weight_scales[:].rearrange("p g n -> p (g n)").bitcast(I32), 0)
@@ -69,14 +69,14 @@ def tile_moe_shr_lin_relu2_kernel(
         def cast_args(q, t0, t1):
             return (
                 pairs[:, q, 2 * t0 : 2 * t1].rearrange("p (t j) -> p t j", j=2),
-                raw[:, q, :, t0:t1].rearrange("p j t -> p t j"),
+                raw[q][:, :, t0:t1].rearrange("p j t -> p t j"),
             )
 
         for t0, t1 in head_pieces:
             nc.vector.tensor_copy(*cast_args(0, t0, t1))
         singles = keep.tile([P, 2, T], BF16, name="singles")
-        nc.scalar.copy(singles[:, 0], raw[:, 1, 0])
-        nc.gpsimd.tensor_scalar(singles[:, 1], raw[:, 1, 1], 1.0, 0.0, ALU.mult, ALU.add)
+        nc.scalar.copy(singles[:, 0], raw[1][:, 0])
+        nc.gpsimd.tensor_scalar(singles[:, 1], raw[1][:, 1], 1.0, 0.0, ALU.mult, ALU.add)
         for q in (2, 3, 1):
             nc.gpsimd.tensor_scalar(*cast_args(q, 0, T), 1.0, 0.0, ALU.mult, ALU.add)
 
@@ -165,51 +165,48 @@ def tile_moe_shr_lin_relu2_kernel(
 
         shared_quads = {}
 
-        def lay_out_shared(a, tag):
-            shared_quads[a] = keep.tile([P, 4 * T], BF16, name="shared_quads%d" % a, tag=tag, align_bytes=64)
-            interleave(nc.gpsimd.tensor_copy, U32, shared_quads[a][:], pairs[:, 2 * a : 2 * a + 2, : 2 * T])
+        def lay_out_shared(a, lo, hi, tag):
+            tile = keep.tile([P, 4 * (hi - lo)], BF16, name="shared_quads%d_%d" % (a, lo), tag=tag, align_bytes=64)
+            shared_quads[a, lo] = tile
+            interleave(nc.gpsimd.tensor_copy, U32, tile[:], pairs[:, 2 * a : 2 * a + 2, 2 * lo : 2 * hi])
 
-        for c in range(3):
+        for c in range(4):
             open_chunk(c, (0, 1), "picked%d" % c)
-        lay_out_shared(0, "shared_quads0")
-        for c, q in ((0, 0), (1, 0), (2, 0), (0, 2), (1, 2), (0, 3), (1, 3), (2, 2), (2, 3)):
+        open_chunk(4, (0,), "raw1")
+        lay_out_shared(0, 0, T, "shared_quads0")
+        lay_out_shared(1, 256, T, "shared_quads1")
+        for c in range(4):
+            gather(c, 0)
+        for c, q in ((0, 2), (1, 2), (0, 3), (1, 3), (2, 2), (2, 3), (3, 2), (3, 3)):
             gather(c, q)
             if q == 3:
                 interleave_gpsimd(c, 1)
+        gather(3, 1)
+        gather(4, 0)
+        gather(4, 1)
         gather_singles(0)
-        gather_singles(1)
-        interleave_scalar(0, 0)
-        gather_singles(2)
-        interleave_scalar(1, 0)
+        for c in range(4):
+            if c < 3:
+                gather_singles(c + 1)
+            interleave_scalar(c, 0)
+        interleave_scalar(4, 0)
 
         quantize_chunk(0)
-        lay_out_shared(1, "quads0")
-        open_chunk(3, (0, 1), "picked0")
-        for q in (0, 2, 3):
-            gather(3, q)
-        interleave_gpsimd(3, 1)
-        gather_singles(3)
-        interleave_scalar(2, 0)
-        interleave_scalar(3, 0)
-
         quantize_chunk(1)
-        open_chunk(4, (0, 1), "picked1")
-        for q in (0, 2, 3):
-            gather(4, q)
+        lay_out_shared(1, 0, 256, "quads1")
+        open_chunk(4, (1,), "picked1")
+        gather(4, 2)
+        gather(4, 3)
         interleave_gpsimd(4, 1)
-        gather_singles(4)
-        experts(0)
-        interleave_scalar(4, 0)
 
         quantize_chunk(2)
         open_chunk(5, (0,), "picked2")
         gather(5, 0)
         gather(5, 1)
         interleave_gpsimd(5, 0)
-        experts(1)
 
         quantize_chunk(3)
-        open_chunk(5, (1,), "picked0")
+        open_chunk(5, (1,), "picked3")
         gather(5, 2)
         gather(5, 3)
         quantize_chunk(4)
@@ -217,13 +214,13 @@ def tile_moe_shr_lin_relu2_kernel(
         operand_tiles(last, CHUNKS[last], "codes%d" % last)
         for a in range(PASSES):
             quantize(last, a * CHUNKS[last], (a + 1) * CHUNKS[last], quads[last][:, a])
-        for c in range(2, len(CHUNKS)):
+        for c in range(len(CHUNKS)):
             experts(c)
 
         operand_tiles("shared", T, "codes4")
-        for a in range(PASSES):
-            for lo, hi in ((0, 512), (512, T)):
-                quantize("shared", a * T + lo, a * T + hi, shared_quads[a][:, 4 * lo : 4 * hi])
+        for a, first, lo, hi in ((0, 0, 0, 512), (0, 0, 512, T), (1, 0, 0, 256), (1, 256, 256, 512), (1, 256, 512, T)):
+            values = shared_quads[a, first][:, 4 * (lo - first) : 4 * (hi - first)]
+            quantize("shared", a * T + lo, a * T + hi, values)
         ys = keep.tile([P, T], F32, name="ys")
         rect_shared = keep.tile([P, T], F32, name="rect_shared")
         for i, (lo, hi) in enumerate(((0, 512), (512, T))):

from contextlib import ExitStack

import concourse.mybir as mybir
from concourse.masks import make_identity

K, T, E, C, N = 1024, 640, 20, 128, 128
TOP = 4
FLOPS = 2 * K * N * (E * C + T)

F32 = mybir.dt.float32
BF16 = mybir.dt.bfloat16
I32 = mybir.dt.int32
U32 = mybir.dt.uint32
U16 = mybir.dt.uint16
U8 = mybir.dt.uint8
FP8X4 = mybir.dt.float8_e4m3fn_x4
FP4X4 = mybir.dt.float4_e2m1fn_x4
ACT = mybir.ActivationFunctionType
ALU = mybir.AluOpType

P = 128
PASSES = 2
WINDOW = 704
CHUNKS = [512, 512, 512, 512, 256, 256]
SCALAR_EXPERTS = 14


def tile_moe_shr_lin_relu2_kernel(
    tc, xT, w_words, w_scales, b, gate, offs, pos1, pos2, pos3, pos4, out
):
    nc = tc.nc
    with ExitStack() as ctx:
        keep = ctx.enter_context(tc.tile_pool(name="keep", bufs=1))
        psum = ctx.enter_context(tc.psum_pool(name="psum", bufs=1))

        slot_list = keep.tile([P, E * C // 16], U16, name="slot_list")
        back_lists = [keep.tile([P, T // 16], U16, name="back_list%d" % r) for r in range(TOP)]
        raw = [keep.tile([P, 2, T], F32, name="raw%d" % q, tag="raw%d" % q) for q in range(4)]
        pairs = keep.tile([P, 4, 2 * WINDOW], BF16, name="pairs", align_bytes=64)
        weights = keep.tile([P, (E + 1) * PASSES, 2 * N], U8, name="weights", align_bytes=64)
        weight_scales = keep.tile([P, (E + 1) * PASSES, N], U8, name="weight_scales", align_bytes=64)
        bias = keep.tile([P, E + 1], F32, name="bias")
        gates = keep.tile([P, TOP, T], F32, name="gates")
        y = keep.tile([P, E * C], F32, name="y")

        rows = xT.rearrange("(a p u j) t -> p a u j t", a=PASSES, u=2, j=2)
        head_pieces = ((0, 448), (448, T))
        for t0, t1 in head_pieces:
            nc.sync.dma_start(out=raw[0][:, :, t0:t1], in_=rows[:, 0, 0, :, t0:t1])
        nc.sync.dma_start(slot_list[:], offs)
        for q in range(1, 4):
            nc.sync.dma_start(out=raw[q][:], in_=rows[:, q // 2, q % 2])

        nc.vector.memset(pairs[:, :, 2 * T :].bitcast(U32), 0)
        nc.vector.memset(weight_scales[:].rearrange("p g n -> p (g n)").bitcast(I32), 0)
        scale_rows = w_scales.rearrange("e a q n -> q (e a) n").bitcast(I32)
        for quad in range(4):
            nc.sync.dma_start(
                out=weight_scales[32 * quad : 32 * quad + 4].bitcast(I32), in_=scale_rows[4 * quad : 4 * quad + 4]
            )
        word_rows = w_words.rearrange("e a p c -> p (e a) c").bitcast(I32)
        for g0, g1 in ((0, 16), (16, 32), (32, 42)):
            nc.sync.dma_start(out=weights[:, g0:g1].bitcast(I32), in_=word_rows[:, g0:g1])
        nc.sync.dma_start(out=bias[:], in_=b)
        for r, pos in enumerate((pos1, pos2, pos3, pos4)):
            nc.sync.dma_start(back_lists[r][:], pos)
        nc.sync.dma_start(out=gates[:], in_=gate.rearrange("r p t -> p r t"))

        def cast_args(q, t0, t1):
            return (
                pairs[:, q, 2 * t0 : 2 * t1].rearrange("p (t j) -> p t j", j=2),
                raw[q][:, :, t0:t1].rearrange("p j t -> p t j"),
            )

        for t0, t1 in head_pieces:
            nc.vector.tensor_copy(*cast_args(0, t0, t1))
        singles = keep.tile([P, 2, T], BF16, name="singles")
        nc.scalar.copy(singles[:, 0], raw[1][:, 0])
        nc.gpsimd.tensor_scalar(singles[:, 1], raw[1][:, 1], 1.0, 0.0, ALU.mult, ALU.add)
        for q in (2, 3, 1):
            nc.gpsimd.tensor_scalar(*cast_args(q, 0, T), 1.0, 0.0, ALU.mult, ALU.add)

        identity = keep.tile([P, P], F32, name="identity")
        make_identity(nc, identity[:])

        starts = [sum(CHUNKS[:c]) for c in range(len(CHUNKS))]
        last = len(CHUNKS) - 1
        picked, quads, codes, scales = {}, {}, {}, {}

        def open_chunk(c, passes, tag):
            tile = keep.tile([P, 2 * len(passes), 2 * CHUNKS[c]], BF16, name="picked%d_%d" % (c, passes[0]), tag=tag)
            for i, a in enumerate(passes):
                picked[c, a] = tile[:, 2 * i : 2 * i + 2]
            if 0 in passes:
                quads[c] = keep.tile(
                    [P, PASSES, 4 * CHUNKS[c]], BF16, name="quads%d" % c, tag="quads%d" % c, align_bytes=64
                )

        def on_scalar(c):
            return min(CHUNKS[c], max(0, SCALAR_EXPERTS * C - starts[c]))

        def gather(c, q):
            skip = on_scalar(c) if q == 1 else 0
            first, end = starts[c] + skip, starts[c] + CHUNKS[c]
            nc.vector.tensor_copy(
                picked[c, q // 2][:, q % 2].bitcast(U32)[:, skip:],
                pairs[:, q].bitcast(U32).indirect(slot_list[:, first // 16 : end // 16]),
            )

        def gather_singles(c):
            slots = picked[c, 0][:, 1].rearrange("p (s j) -> p s j", j=2)
            for s0 in range(0, on_scalar(c), C):
                first = starts[c] + s0
                for j in range(2):
                    window = singles[:, j].indirect(slot_list[:, first // 16 : (first + C) // 16])
                    nc.scalar.activation(slots[:, s0 : s0 + C, j], window, ACT.Copy)

        def interleave(copy, word, dst, src):
            copy(dst.bitcast(word).rearrange("p (s u) -> p s u", u=2), src.bitcast(word).rearrange("p u s -> p s u"))

        def interleave_scalar(c, a):
            interleave(nc.scalar.copy, F32, quads[c][:, a], picked[c, a])

        def interleave_gpsimd(c, a):
            interleave(nc.gpsimd.tensor_copy, U32, quads[c][:, a], picked[c, a])

        def interleave_vector(c, a):
            interleave(nc.vector.tensor_copy, I32, quads[c][:, a], picked[c, a])

        def operand_tiles(key, width, tag):
            codes[key] = keep.tile([P, PASSES * width], U32, name="codes%s" % key, tag=tag, align_bytes=64)
            scales[key] = keep.tile([P, PASSES * width], U8, name="scales%s" % key, align_bytes=64)

        def quantize(key, lo, hi, values):
            nc.vector.quantize_mx(out=codes[key][:, lo:hi].bitcast(FP8X4), scales=scales[key][:, lo:hi], in_=values)

        def quantize_chunk(c):
            operand_tiles(c, CHUNKS[c], "codes%d" % c)
            quantize(c, 0, PASSES * CHUNKS[c], quads[c][:].rearrange("p a s -> p (a s)"))

        def product(acc, e, key, width, lo, hi):
            for a in range(PASSES):
                cols = slice(a * width + lo, a * width + hi)
                nc.tensor.matmul_mx(
                    out=acc,
                    lhsT=weights[:, PASSES * e + a].bitcast(FP4X4),
                    lhsT_scale=weight_scales[:, PASSES * e + a],
                    rhs=codes[key][:, cols].bitcast(FP8X4),
                    rhs_scale=scales[key][:, cols],
                    start=(a == 0),
                    stop=(a == PASSES - 1),
                )

        def experts(c):
            s = CHUNKS[c]
            acc = psum.tile([P, s], F32, name="acc%d" % c, tag="bank%d" % c)
            rect = keep.tile([P, s], F32, name="rect%d" % c)
            first = starts[c] // C
            for i in range(s // C):
                product(acc[:, i * C : (i + 1) * C], first + i, c, s, i * C, (i + 1) * C)
            for i in range(s // C):
                cols = slice(i * C, (i + 1) * C)
                nc.scalar.activation(rect[:, cols], acc[:, cols], ACT.Relu, bias=bias[:, first + i : first + i + 1])
            nc.scalar.activation(y[:, starts[c] : starts[c] + s], rect[:], ACT.Square)

        shared_quads = {}

        def lay_out_shared(a, lo, hi, tag):
            tile = keep.tile([P, 4 * (hi - lo)], BF16, name="shared_quads%d_%d" % (a, lo), tag=tag, align_bytes=64)
            shared_quads[a, lo] = tile
            interleave(nc.gpsimd.tensor_copy, U32, tile[:], pairs[:, 2 * a : 2 * a + 2, 2 * lo : 2 * hi])

        for c in range(4):
            open_chunk(c, (0, 1), "picked%d" % c)
        open_chunk(4, (0,), "raw1")
        lay_out_shared(0, 0, T, "shared_quads0")
        lay_out_shared(1, 256, T, "shared_quads1")
        for c in range(4):
            gather(c, 0)
        for c, q in ((0, 2), (1, 2), (0, 3), (1, 3), (2, 2), (2, 3), (3, 2), (3, 3)):
            gather(c, q)
            if q == 3:
                interleave_gpsimd(c, 1)
        gather(3, 1)
        gather(4, 0)
        gather(4, 1)
        gather_singles(0)
        for c in range(4):
            if c < 3:
                gather_singles(c + 1)
            interleave_scalar(c, 0)
        interleave_scalar(4, 0)

        quantize_chunk(0)
        quantize_chunk(1)
        lay_out_shared(1, 0, 256, "quads1")
        open_chunk(4, (1,), "picked1")
        gather(4, 2)
        gather(4, 3)
        interleave_gpsimd(4, 1)

        quantize_chunk(2)
        open_chunk(5, (0,), "picked2")
        gather(5, 0)
        gather(5, 1)
        interleave_gpsimd(5, 0)

        quantize_chunk(3)
        open_chunk(5, (1,), "picked3")
        gather(5, 2)
        gather(5, 3)
        quantize_chunk(4)
        interleave_vector(5, 1)
        operand_tiles(last, CHUNKS[last], "codes%d" % last)
        for a in range(PASSES):
            quantize(last, a * CHUNKS[last], (a + 1) * CHUNKS[last], quads[last][:, a])
        for c in range(len(CHUNKS)):
            experts(c)

        operand_tiles("shared", T, "codes4")
        for a, first, lo, hi in ((0, 0, 0, 512), (0, 0, 512, T), (1, 0, 0, 256), (1, 256, 256, 512), (1, 256, 512, T)):
            values = shared_quads[a, first][:, 4 * (lo - first) : 4 * (hi - first)]
            quantize("shared", a * T + lo, a * T + hi, values)
        ys = keep.tile([P, T], F32, name="ys")
        rect_shared = keep.tile([P, T], F32, name="rect_shared")
        for i, (lo, hi) in enumerate(((0, 512), (512, T))):
            acc = psum.tile([P, hi - lo], F32, name="acc_shared%d" % i, tag="bank%d" % (6 + i))
            product(acc[:], E, "shared", T, lo, hi)
            nc.scalar.activation(rect_shared[:, lo:hi], acc[:], ACT.Relu, bias=bias[:, E : E + 1])
        token_pieces = ((0, 384), (384, T))
        for lo, hi in token_pieces:
            nc.scalar.activation(ys[:, lo:hi], rect_shared[:, lo:hi], ACT.Square)

        terms = [keep.tile([P, T], F32, name="term%d" % r) for r in range(TOP)]

        def fetch(r, lo, hi):
            window = y[:].indirect(back_lists[r][:, lo // 16 : hi // 16])
            nc.vector.tensor_tensor(terms[r][:, lo:hi], window, gates[:, r, lo:hi], ALU.mult)

        partial = keep.tile([P, T], F32, name="partial")
        result = keep.tile([P, T], F32, name="result")
        addends = [terms[0], terms[1], ys, terms[2]]
        backs = []
        for i, (lo, hi) in enumerate(token_pieces):
            for r in range(TOP - 1):
                fetch(r, lo, hi)
            blocks = range(lo // P, hi // P)
            turned = {k: psum.tile([P, P], F32, name="turned%d" % k, tag="bank%d" % k) for k in blocks}
            for n, addend in enumerate(addends):
                for k in blocks:
                    nc.tensor.matmul(
                        turned[k][:],
                        lhsT=addend[:, k * P : (k + 1) * P],
                        rhs=identity[:],
                        start=(n == 0),
                        stop=(n == len(addends) - 1),
                        is_transpose=True,
                    )
            for k in blocks:
                nc.scalar.copy(partial[:, k * P : (k + 1) * P], turned[k][:])
            back = psum.tile([P, hi - lo], F32, name="back%d" % i, tag="bank%d" % (6 + i))
            for t0 in range(lo, hi, P):
                nc.tensor.transpose(back[:, t0 - lo : t0 - lo + P], partial[:, t0 : t0 + P], identity[:])
            backs.append(back)
        for lo, hi in token_pieces:
            fetch(TOP - 1, lo, hi)
        for back, (lo, hi) in zip(backs, token_pieces):
            nc.vector.tensor_tensor(result[:, lo:hi], back[:], terms[TOP - 1][:, lo:hi], ALU.add)
            nc.sync.dma_start(out=out[:, lo:hi], in_=result[:, lo:hi])
